import numpy as np, ml_dtypes
CORES = [24,40,56,80,88,96]
N = 6
import mx_ref
NC = 512
BF = ml_dtypes.bfloat16
def setup_inputs(rng):
    def f(*shape):
        return mx_ref.flush((rng.standard_normal(shape, dtype=np.float32) * np.exp2(rng.integers(-2, 3, shape[:-1] + (1,)))).astype(BF))
    return {"x": f(N, 128, 512), "rt": f(N, 128, 512), "w": f(N, 128, 4 * NC)}
def setup_inputs_blocks(rng):
    d = setup_inputs(rng)
    for k in ("x", "rt", "w"): d[k] = mx_ref.spread(d[k], rng, 1)
    return d
def setup_inputs_wide(rng):
    d = setup_inputs(rng)
    for k in ("x", "rt", "w"): d[k] = mx_ref.flush((d[k].astype(np.float32) * np.exp2(rng.integers(-6, 7, (N, 1, 1))).astype(np.float32)).astype(BF))
    return d
def setup_inputs_near(rng):
    d = setup_inputs(rng); v = d["rt"].astype(np.float32).reshape(N, 128, -1, 4)
    d["rt"] = mx_ref.flush((v[:, :, :1] + v / 64).reshape(d["rt"].shape).astype(BF))
    return d
def setup_inputs_twins(rng):
    d = setup_inputs(rng); v = d["rt"].reshape(N, 128, -1, 4).copy()
    v[:, :, 1] = v[:, :, 0]
    d["rt"] = v.reshape(d["rt"].shape)
    return d
def reference(x, rt, w):
    W = [mx_ref.quantize(w[e]) for e in range(N)]
    y = np.zeros((N, 128, NC), np.float32)
    for j in range(N):
        X = mx_ref.quantize(x[j])
        lg = mx_ref.matmul(X, mx_ref.quantize(rt[j]))[:, :N]
        m = lg.max(axis=1, keepdims=True); m2 = np.where(lg < m, lg, -np.inf).max(axis=1, keepdims=True)
        for e in range(N):
            y[j] = y[j] + (lg[:, e:e + 1] >= m2) * (mx_ref.matmul(X, W[e]) * lg[:, e:e + 1])
    return {"y": y}

@@ -1,0 +1,217 @@
+from concourse.bass import DstId, RemoteDMATransfer
+from concourse.mybir import dt, AluOpType, AxisListType, ActivationFunctionType
+
+N = 6
+NC = 512
+H = NC // 2
+BIG = 1.0e29
+
+SCRATCH = {
+    "wb": ("sbuf", [128, 4 * NC], "bfloat16"),
+    "xb": ("sbuf", [128, 512], "bfloat16"),
+    "rb": ("sbuf", [128, 512], "bfloat16"),
+    "wq": ("sbuf", [128, N * NC], "float8_e4m3fn_x4"),
+    "ws": ("sbuf", [128, N * NC], "uint8"),
+    "xq": ("sbuf", [128, 128], "float8_e4m3fn_x4"),
+    "xs": ("sbuf", [128, 128], "uint8"),
+    "rq": ("sbuf", [128, 128], "float8_e4m3fn_x4"),
+    "rs": ("sbuf", [128, 128], "uint8"),
+    "m1": ("sbuf", [128, 4], "float32"),
+    "m2": ("sbuf", [128, 4], "float32"),
+    "pen": ("sbuf", [128, 8], "float32"),
+    "msk": ("sbuf", [128, 8], "float32"),
+    "sel": ("sbuf", [128, 8], "float32"),
+    "gate": ("sbuf", [128, 8], "float32"),
+    "p": ("sbuf", [128, N * NC], "float32"),
+    "acc": ("sbuf", [128, NC], "float32"),
+    "lg": ("psum", [128, 512], "float32"),
+    "ps": ("psum", [128, 512 * 7], "float32"),
+}
+PIECES = 2 * N
+SEMAPHORES = (["lwa", "lwb", "lx", "lr", "qw", "qx", "tl", "vg", "gt", "va", "hc", "hs", "sent", "sta", "stb"]
+              + ["a%d" % e for e in range(N)] + ["b%d" % e for e in range(N)]
+              + ["mm%d" % k for k in range(PIECES)] + ["pr%d" % k for k in range(PIECES)])
+HALVES = {"a": (0, H), "b": (H, NC), "ab": (0, NC)}
+
+
+def engine_groups(mask, parts):
+    bits = [i for i in range(16) if mask >> i & 1]
+    n = len(bits) // parts
+    return [sum(1 << i for i in bits[k * n:(k + 1) * n]) for k in range(parts)]
+
+
+def count(mask):
+    return bin(mask).count("1")
+
+
+def make_plan(T, topo):
+    plan = []
+    for e in range(N):
+        c = T.cores[e]
+        others = [T.cores[(e + k) % N] for k in range(1, N)]
+        chip = topo.chip(c)
+        near = [d for d in others if topo.same_plane(chip, topo.chip(d))]
+        far = [d for d in others if d not in near]
+        local = [h for h in range(c - 8 if c > 8 else 0, c + 8) if topo.chip(h) == chip and h != c]
+        ports = [h for h in local if all(topo.may_write(h, d) for d in far)]
+        plain = [h for h in local if h not in ports]
+        pa = [h for h in ports if topo.die(h) == topo.die(c)]
+        pb = [h for h in ports if topo.die(h) != topo.die(c)]
+        nb = [h for h in plain if topo.die(h) != topo.die(c)]
+        if len(far) <= 2:
+            copies = [(pa[0], "a"), (pb[0], "b"), (nb[0], "b"), (nb[1], "b")]
+            sends = {c: ("a", near), pa[0]: ("a", far), pb[0]: ("b", far), nb[0]: ("b", near[:2]), nb[1]: ("b", near[2:])}
+        else:
+            copies = [(pa[0], "a"), (pa[1], "a"), (pb[0], "b"), (pb[1], "b")]
+            sends = {c: ("ab", near), pa[0]: ("a", far[:2]), pa[1]: ("a", far[2:]), pb[0]: ("b", far[:2]), pb[1]: ("b", far[2:])}
+        plan.append((copies, sends))
+    return plan
+
+
+def views(T, e, half):
+    lo, hi = HALVES[half]
+    lo, hi = e * NC + lo, e * NC + hi
+    return T.wq[:, lo:hi].bitcast(dt.uint8), T.ws[:, lo:hi]
+
+
+def dst_id(topo, d):
+    rid, pid, _ = topo.addr(d)
+    return DstId(rid=rid, pnc=pid)
+
+
+def send_layout(src, dests, topo):
+    m = topo.mask(src, dests[0])
+    if len(dests) == 2:
+        return [([d], k) for d, k in zip(dests, engine_groups(m, 2))]
+    return [(dests, m)]
+
+
+def emit_send(g, T, topo, src, e, half, dests, which, sem):
+    v = views(T, e, half)[which]
+    tr = [RemoteDMATransfer(dst_ids=[dst_id(topo, d) for d in ds], dma_engine_mask=m, remote_sem=sem,
+                            srcs=[v], dsts=[v for _ in ds]) for ds, m in send_layout(src, dests, topo)]
+    g.remote_dma_fused(tr, local_sem=T.sem["sent"])
+    return sum(count(t) for _, t in send_layout(src, dests, topo))
+
+
+def arrival(T, topo, plan, e, core):
+    out = []
+    for src, (half, dests) in plan[e][1].items():
+        if core in dests:
+            m = [m for ds, m in send_layout(src, dests, topo) if core in ds][0]
+            out.append((half, count(m), src == T.cores[e]))
+    return sorted(out)
+
+
+def rank_program(g, core, T, topo):
+    plan = make_plan(T, topo)
+    rank = T.rank_of(core)
+    if rank is None:
+        for e in range(N):
+            copies, sends = plan[e]
+            if core in sends:
+                helper(g, core, T, topo, e, len(copies), sends[core])
+        return
+    e = rank
+    copies, sends = plan[e]
+
+    g.sync.dma_start(T.wb[:, 0:4 * H], T.w[:, 0:4 * H]).then_inc(T.sem["lwa"], 16)
+    g.scalar.dma_start(T.wb[:, 4 * H:4 * NC], T.w[:, 4 * H:4 * NC]).then_inc(T.sem["lwb"], 16)
+    g.sync.dma_start(T.xb[:], T.x[:]).then_inc(T.sem["lx"], 16)
+    g.scalar.dma_start(T.rb[:], T.rt[:]).then_inc(T.sem["lr"], 16)
+
+    v = g.vector
+    for half, sem in (("a", "lwa"), ("b", "lwb")):
+        lo, hi = HALVES[half]
+        v.wait_ge(T.sem[sem], 16)
+        v.quantize_mx(T.wq[:, e * NC + lo:e * NC + hi], T.ws[:, e * NC + lo:e * NC + hi],
+                      T.wb[:, 4 * lo:4 * hi]).then_inc(T.sem["qw"], 1)
+    v.wait_ge(T.sem["lx"], 16)
+    v.quantize_mx(T.xq[:], T.xs[:], T.xb[:]).then_inc(T.sem["qx"], 1)
+    v.wait_ge(T.sem["lr"], 16)
+    v.quantize_mx(T.rq[:], T.rs[:], T.rb[:]).then_inc(T.sem["qx"], 1)
+
+    g.wait_ge(T.sem["qw"], 2)
+    total = 0
+    for which, sem in ((0, "hc"), (1, "hs")):
+        groups = engine_groups(topo.mask(core, copies[0][0]), len(copies))
+        tr = []
+        for (h, half), m in zip(copies, groups):
+            vw = views(T, e, half)[which]
+            tr.append(RemoteDMATransfer(dst_ids=[dst_id(topo, h)], dma_engine_mask=m, remote_sem=T.sem[sem],
+                                        srcs=[vw], dsts=[vw]))
+            total += count(m)
+        g.remote_dma_fused(tr, local_sem=T.sem["sent"])
+    half, dests = sends[core]
+    for which in (0, 1):
+        total += emit_send(g, T, topo, core, e, half, dests, which, T.sem[half[0] + str(e)])
+    g.wait_ge(T.sem["sent"], total)
+
+    own = (e, 0, NC, "qw", 2)
+    first, second, last = [], [], []
+    for k in range(1, N):
+        s = (e - k) % N
+        plane = topo.same_plane(topo.chip(T.cores[s]), topo.chip(core))
+        for half_, n, direct in arrival(T, topo, plan, s, core):
+            lo, hi = HALVES[half_]
+            (first if direct else second if plane else last).append((s, lo, hi, half_[0] + str(s), 2 * n))
+    pieces = [own] + first + second + last
+
+    t = g.tensor
+    t.wait_ge(T.sem["qx"], 2)
+    t.matmul_mx(T.lg[:, 0:128], T.xq[:], T.xs[:], T.rq[:], T.rs[:], True, True).then_inc(T.sem["tl"], 1)
+    for k, (s, lo, hi, sem, n) in enumerate(pieces):
+        t.wait_ge(T.sem[sem], n)
+        if k >= 7:
+            t.wait_ge(T.sem["pr%d" % (k - 7)], 1)
+        b = 512 * (k % 7)
+        t.matmul_mx(T.ps[:, b:b + hi - lo], T.xq[:], T.xs[:], T.wq[:, s * NC + lo:s * NC + hi],
+                    T.ws[:, s * NC + lo:s * NC + hi], True, True).then_inc(T.sem["mm%d" % k], 1)
+
+    lg = T.lg[:, 0:N]
+    v.wait_ge(T.sem["tl"], 1)
+    v.tensor_reduce(T.m1[:, 0:1], lg, AxisListType.X, AluOpType.max).then_inc(T.sem["vg"], 1)
+    v.wait_ge(T.sem["vg"], 1)
+    v.tensor_scalar(T.pen[:, 0:N], lg, T.m1[:, 0:1], BIG, AluOpType.is_equal, AluOpType.mult).then_inc(T.sem["vg"], 1)
+    v.wait_ge(T.sem["vg"], 2)
+    v.tensor_tensor(T.msk[:, 0:N], lg, T.pen[:, 0:N], AluOpType.subtract).then_inc(T.sem["vg"], 1)
+    v.wait_ge(T.sem["vg"], 3)
+    v.tensor_reduce(T.m2[:, 0:1], T.msk[:, 0:N], AxisListType.X, AluOpType.max).then_inc(T.sem["vg"], 1)
+    v.wait_ge(T.sem["vg"], 4)
+    v.tensor_scalar(T.sel[:, 0:N], lg, T.m2[:, 0:1], None, AluOpType.is_ge).then_inc(T.sem["vg"], 1)
+    v.wait_ge(T.sem["vg"], 5)
+    v.tensor_tensor(T.gate[:, 0:N], lg, T.sel[:, 0:N], AluOpType.mult).then_inc(T.sem["gt"], 1)
+
+    g.scalar.wait_ge(T.sem["gt"], 1)
+    for k, (s, lo, hi, sem, n) in enumerate(pieces):
+        g.scalar.wait_ge(T.sem["mm%d" % k], 1)
+        b = 512 * (k % 7)
+        out = T.acc[:, lo:hi] if k == 0 else T.p[:, s * NC + lo:s * NC + hi]
+        g.scalar.activation(out, T.ps[:, b:b + hi - lo], ActivationFunctionType.Copy,
+                            scale=T.gate[:, s:s + 1]).then_inc(T.sem["pr%d" % k], 1)
+    done = {0: 0, H: 0}
+    v.wait_ge(T.sem["pr0"], 1)
+    for k, (s, lo, hi, sem, n) in enumerate(pieces[1:], 1):
+        v.wait_ge(T.sem["pr%d" % k], 1)
+        if k > 1:
+            v.wait_ge(T.sem["va"], k - 1)
+        v.tensor_tensor(T.acc[:, lo:hi], T.acc[:, lo:hi], T.p[:, s * NC + lo:s * NC + hi],
+                        AluOpType.add).then_inc(T.sem["va"], 1)
+        for c0 in done:
+            if lo <= c0 < hi:
+                done[c0] = k
+    for c0, q, sem in ((0, g.sync, "sta"), (H, g.scalar, "stb")):
+        q.wait_ge(T.sem["va"], done[c0])
+        q.dma_start(T.y[:, c0:c0 + H], T.acc[:, c0:c0 + H]).then_inc(T.sem[sem], 16)
+        q.wait_ge(T.sem[sem], 16)
+    v.wait_ge(T.sem["va"], len(pieces) - 1)
+
+
+def helper(g, core, T, topo, e, ncopies, send):
+    half, dests = send
+    n = count(topo.mask(T.cores[e], core)) // ncopies
+    total = 0
+    for which, sem in ((0, "hc"), (1, "hs")):
+        g.wait_ge(T.sem[sem], n)
+        total += emit_send(g, T, topo, core, e, half, dests, which, T.sem[half + str(e)])
+    g.wait_ge(T.sem["sent"], total)

@@ -4,6 +4,8 @@ from concourse.mybir import dt, AluOpType, AxisListType, ActivationFunctionType
 N = 6
 NC = 512
 H = NC // 2
+Q = NC // 4
+NCORES = 112
 BIG = 1.0e29
 
 SCRATCH = {
@@ -28,16 +30,15 @@ SCRATCH = {
     "ps": ("psum", [128, 512 * 7], "float32"),
 }
 PIECES = 2 * N
-SEMAPHORES = (["lwa", "lwb", "lx", "lr", "qw", "qx", "tl", "vg", "gt", "va", "hc", "hs", "sent", "sta", "stb"]
-              + ["a%d" % e for e in range(N)] + ["b%d" % e for e in range(N)]
+SEMAPHORES = (["lwa", "lwb", "lx", "lr", "qa", "qb", "qx", "tl", "vg", "gt", "va", "sent", "sta", "stb"]
+              + ["%s%d" % (u, e) for u in "abs" for e in range(N)]
               + ["mm%d" % k for k in range(PIECES)] + ["pr%d" % k for k in range(PIECES)])
-HALVES = {"a": (0, H), "b": (H, NC), "ab": (0, NC)}
+LANDS = {"c0": "a", "c1": "a", "c2": "b", "c3": "b", "s": "s"}
 
 
-def engine_groups(mask, parts):
+def groups(mask, parts):
     bits = [i for i in range(16) if mask >> i & 1]
-    n = len(bits) // parts
-    return [sum(1 << i for i in bits[k * n:(k + 1) * n]) for k in range(parts)]
+    return [sum(1 << i for i in bits[k::parts]) for k in range(parts)]
 
 
 def count(mask):
@@ -45,33 +46,70 @@ def count(mask):
 
 
 def make_plan(T, topo):
+    rank_chips = [topo.chip(c) for c in T.cores]
+    taken, used = set(T.cores), set()
     plan = []
+
+    def pick(cand):
+        h = [h for h in cand if h not in taken][-1]
+        taken.add(h)
+        return h
+
     for e in range(N):
         c = T.cores[e]
-        others = [T.cores[(e + k) % N] for k in range(1, N)]
         chip = topo.chip(c)
+        others = [T.cores[(e + k) % N] for k in range(1, N)]
         near = [d for d in others if topo.same_plane(chip, topo.chip(d))]
         far = [d for d in others if d not in near]
-        local = [h for h in range(c - 8 if c > 8 else 0, c + 8) if topo.chip(h) == chip and h != c]
+        local = [h for h in range(NCORES) if topo.chip(h) == chip and h != c]
         ports = [h for h in local if all(topo.may_write(h, d) for d in far)]
-        plain = [h for h in local if h not in ports]
         pa = [h for h in ports if topo.die(h) == topo.die(c)]
         pb = [h for h in ports if topo.die(h) != topo.die(c)]
-        nb = [h for h in plain if topo.die(h) != topo.die(c)]
-        if len(far) <= 2:
-            copies = [(pa[0], "a"), (pb[0], "b"), (nb[0], "b"), (nb[1], "b")]
-            sends = {c: ("a", near), pa[0]: ("a", far), pb[0]: ("b", far), nb[0]: ("b", near[:2]), nb[1]: ("b", near[2:])}
+        nb = [h for h in local if h not in ports and topo.die(h) != topo.die(c)]
+        relay = {}
+        for d in far:
+            if not any(topo.mates(topo.chip(d), r) for r in rank_chips):
+                relay[d] = pick([h for h in range(NCORES) if topo.mates(topo.chip(h), topo.chip(d))
+                                 and topo.may_write(h, d) and topo.may_write(c, h)])
+        rest = [d for d in far if d not in relay]
+        on, out = topo.mask(c, pa[0]), topo.mask(c, near[0])
+        if len(near) == 1:
+            idle = [h for h in range(NCORES) if topo.same_plane(topo.chip(h), chip) and topo.chip(h) not in used
+                    and not any(r == topo.chip(h) or topo.mates(r, topo.chip(h)) for r in rank_chips)
+                    and all(topo.may_write(h, d) for d in far)]
+            h0 = pick([h for h in idle if topo.die(h) != topo.die(c)])
+            h2 = pick([h for h in idle if topo.chip(h) == topo.chip(h0) and topo.die(h) == topo.die(c)])
+            used.add(topo.chip(h0))
+            keeper, to0 = pa[0], far
+            m0, m1 = groups(out, 2)
+            m2, m3 = groups(on & ~out, 2)
+            first = [("c0", m0, [h0]), ("c1", m1 | m2, [pb[0]])]
+            second = [("c2", m0, [h2]), ("c3", m1, [pb[1]]), ("s", m2, [keeper]), ("c3", m3, [nb[0]])]
+            last = [("c2", m0, near), ("c0", m1, near)]
         else:
-            copies = [(pa[0], "a"), (pa[1], "a"), (pb[0], "b"), (pb[1], "b")]
-            sends = {c: ("ab", near), pa[0]: ("a", far[:2]), pa[1]: ("a", far[2:]), pb[0]: ("b", far[:2]), pb[1]: ("b", far[2:])}
-        plan.append((copies, sends))
+            h0, h2, keeper, to0 = pa[0], pa[1], pb[1], others
+            g2, g4 = groups(on, 2), groups(on, 4)
+            first = [("c0", g2[0], [h0]), ("c1", g2[1], [pb[0]])]
+            second = [("c2", g4[0], [h2]), ("c3", g4[1], [pb[1]]), ("s", g4[2], [keeper]), ("c3", g4[3], [nb[0]])]
+            last = [("c2", out, near)]
+        calls = {c: [first, second, [("s", out, list(relay.values()) + near)], last]}
+        calls[h0] = [[("c0", out, to0)]]
+        calls[pb[0]] = [[("c1", out, others)]]
+        calls[h2] = [[("c2", out, far)]]
+        calls[pb[1]] = [[("c3", out, far)]]
+        calls[nb[0]] = [[("c3", out, near)]]
+        calls.setdefault(keeper, []).append([("s", out, rest)])
+        for d, h in relay.items():
+            calls[h] = [[("s", topo.mask(h, d), [d])]]
+        plan.append(calls)
     return plan
 
 
-def views(T, e, half):
-    lo, hi = HALVES[half]
-    lo, hi = e * NC + lo, e * NC + hi
-    return T.wq[:, lo:hi].bitcast(dt.uint8), T.ws[:, lo:hi]
+def view(T, e, unit):
+    if unit == "s":
+        return T.ws[:, e * NC:(e + 1) * NC]
+    lo = e * NC + Q * int(unit[1])
+    return T.wq[:, lo:lo + Q].bitcast(dt.uint8)
 
 
 def dst_id(topo, d):
@@ -79,28 +117,29 @@ def dst_id(topo, d):
     return DstId(rid=rid, pnc=pid)
 
 
-def send_layout(src, dests, topo):
-    m = topo.mask(src, dests[0])
-    if len(dests) == 2:
-        return [([d], k) for d, k in zip(dests, engine_groups(m, 2))]
-    return [(dests, m)]
+def semaphore(e, unit):
+    return LANDS[unit] + str(e)
 
 
-def emit_send(g, T, topo, src, e, half, dests, which, sem):
-    v = views(T, e, half)[which]
-    tr = [RemoteDMATransfer(dst_ids=[dst_id(topo, d) for d in ds], dma_engine_mask=m, remote_sem=sem,
-                            srcs=[v], dsts=[v for _ in ds]) for ds, m in send_layout(src, dests, topo)]
+def issue(g, T, topo, e, call):
+    tr = []
+    for unit, mask, dests in call:
+        v = view(T, e, unit)
+        tr.append(RemoteDMATransfer(dst_ids=[dst_id(topo, d) for d in dests], dma_engine_mask=mask,
+                                    remote_sem=T.sem[semaphore(e, unit)], srcs=[v], dsts=[v for _ in dests]))
     g.remote_dma_fused(tr, local_sem=T.sem["sent"])
-    return sum(count(t) for _, t in send_layout(src, dests, topo))
+    return sum(count(m) for _, m, _ in call)
 
 
-def arrival(T, topo, plan, e, core):
-    out = []
-    for src, (half, dests) in plan[e][1].items():
-        if core in dests:
-            m = [m for ds, m in send_layout(src, dests, topo) if core in ds][0]
-            out.append((half, count(m), src == T.cores[e]))
-    return sorted(out)
+def landing(calls, e, core):
+    got = {}
+    for cs in calls.values():
+        for call in cs:
+            for unit, mask, dests in call:
+                if core in dests:
+                    s = semaphore(e, unit)
+                    got[s] = got.get(s, 0) + count(mask)
+    return got
 
 
 def rank_program(g, core, T, topo):
@@ -108,60 +147,51 @@ def rank_program(g, core, T, topo):
     rank = T.rank_of(core)
     if rank is None:
         for e in range(N):
-            copies, sends = plan[e]
-            if core in sends:
-                helper(g, core, T, topo, e, len(copies), sends[core])
+            if core in plan[e]:
+                helper(g, core, T, topo, e, plan[e])
         return
     e = rank
-    copies, sends = plan[e]
 
-    g.sync.dma_start(T.wb[:, 0:4 * H], T.w[:, 0:4 * H]).then_inc(T.sem["lwa"], 16)
-    g.scalar.dma_start(T.wb[:, 4 * H:4 * NC], T.w[:, 4 * H:4 * NC]).then_inc(T.sem["lwb"], 16)
+    for lo, hi, sem in ((0, 4 * H, "lwa"), (4 * H, 4 * NC, "lwb")):
+        g.sync.dma_start(T.wb[0:64, lo:hi], T.w[0:64, lo:hi]).then_inc(T.sem[sem], 16)
+        g.scalar.dma_start(T.wb[64:128, lo:hi], T.w[64:128, lo:hi]).then_inc(T.sem[sem], 16)
     g.sync.dma_start(T.xb[:], T.x[:]).then_inc(T.sem["lx"], 16)
     g.scalar.dma_start(T.rb[:], T.rt[:]).then_inc(T.sem["lr"], 16)
 
     v = g.vector
-    for half, sem in (("a", "lwa"), ("b", "lwb")):
-        lo, hi = HALVES[half]
-        v.wait_ge(T.sem[sem], 16)
-        v.quantize_mx(T.wq[:, e * NC + lo:e * NC + hi], T.ws[:, e * NC + lo:e * NC + hi],
-                      T.wb[:, 4 * lo:4 * hi]).then_inc(T.sem["qw"], 1)
+    for lo, sem, done in ((0, "lwa", "qa"), (H, "lwb", "qb")):
+        v.wait_ge(T.sem[sem], 32)
+        v.quantize_mx(T.wq[:, e * NC + lo:e * NC + lo + H], T.ws[:, e * NC + lo:e * NC + lo + H],
+                      T.wb[:, 4 * lo:4 * (lo + H)]).then_inc(T.sem[done], 1)
     v.wait_ge(T.sem["lx"], 16)
     v.quantize_mx(T.xq[:], T.xs[:], T.xb[:]).then_inc(T.sem["qx"], 1)
     v.wait_ge(T.sem["lr"], 16)
     v.quantize_mx(T.rq[:], T.rs[:], T.rb[:]).then_inc(T.sem["qx"], 1)
 
-    g.wait_ge(T.sem["qw"], 2)
     total = 0
-    for which, sem in ((0, "hc"), (1, "hs")):
-        groups = engine_groups(topo.mask(core, copies[0][0]), len(copies))
-        tr = []
-        for (h, half), m in zip(copies, groups):
-            vw = views(T, e, half)[which]
-            tr.append(RemoteDMATransfer(dst_ids=[dst_id(topo, h)], dma_engine_mask=m, remote_sem=T.sem[sem],
-                                        srcs=[vw], dsts=[vw]))
-            total += count(m)
-        g.remote_dma_fused(tr, local_sem=T.sem["sent"])
-    half, dests = sends[core]
-    for which in (0, 1):
-        total += emit_send(g, T, topo, core, e, half, dests, which, T.sem[half[0] + str(e)])
+    g.wait_ge(T.sem["qa"], 1)
+    for k, call in enumerate(plan[e][core]):
+        if k == 1:
+            g.wait_ge(T.sem["qb"], 1)
+        total += issue(g, T, topo, e, call)
     g.wait_ge(T.sem["sent"], total)
 
-    own = (e, 0, NC, "qw", 2)
-    first, second, last = [], [], []
+    pieces = [(e, 0, NC, [("qa", 1), ("qb", 1)])]
     for k in range(1, N):
         s = (e - k) % N
-        plane = topo.same_plane(topo.chip(T.cores[s]), topo.chip(core))
-        for half_, n, direct in arrival(T, topo, plan, s, core):
-            lo, hi = HALVES[half_]
-            (first if direct else second if plane else last).append((s, lo, hi, half_[0] + str(s), 2 * n))
-    pieces = [own] + first + second + last
+        got = landing(plan[s], s, core)
+        ab = [(s, lo, lo + H, [("s%d" % s, got["s%d" % s]), (n, got[n])]) for lo, n in ((0, "a%d" % s), (H, "b%d" % s))]
+        pieces += ab if k < 3 else ab[::-1]
 
     t = g.tensor
     t.wait_ge(T.sem["qx"], 2)
     t.matmul_mx(T.lg[:, 0:128], T.xq[:], T.xs[:], T.rq[:], T.rs[:], True, True).then_inc(T.sem["tl"], 1)
-    for k, (s, lo, hi, sem, n) in enumerate(pieces):
-        t.wait_ge(T.sem[sem], n)
+    waited = set()
+    for k, (s, lo, hi, sems) in enumerate(pieces):
+        for name, n in sems:
+            if name not in waited:
+                t.wait_ge(T.sem[name], n)
+                waited.add(name)
         if k >= 7:
             t.wait_ge(T.sem["pr%d" % (k - 7)], 1)
         b = 512 * (k % 7)
@@ -183,7 +213,7 @@ def rank_program(g, core, T, topo):
     v.tensor_tensor(T.gate[:, 0:N], lg, T.sel[:, 0:N], AluOpType.mult).then_inc(T.sem["gt"], 1)
 
     g.scalar.wait_ge(T.sem["gt"], 1)
-    for k, (s, lo, hi, sem, n) in enumerate(pieces):
+    for k, (s, lo, hi, sems) in enumerate(pieces):
         g.scalar.wait_ge(T.sem["mm%d" % k], 1)
         b = 512 * (k % 7)
         out = T.acc[:, lo:hi] if k == 0 else T.p[:, s * NC + lo:s * NC + hi]
@@ -191,27 +221,25 @@ def rank_program(g, core, T, topo):
                             scale=T.gate[:, s:s + 1]).then_inc(T.sem["pr%d" % k], 1)
     done = {0: 0, H: 0}
     v.wait_ge(T.sem["pr0"], 1)
-    for k, (s, lo, hi, sem, n) in enumerate(pieces[1:], 1):
+    for k, (s, lo, hi, sems) in enumerate(pieces[1:], 1):
         v.wait_ge(T.sem["pr%d" % k], 1)
-        if k > 1:
-            v.wait_ge(T.sem["va"], k - 1)
+        if done[lo]:
+            v.wait_ge(T.sem["va"], done[lo])
         v.tensor_tensor(T.acc[:, lo:hi], T.acc[:, lo:hi], T.p[:, s * NC + lo:s * NC + hi],
                         AluOpType.add).then_inc(T.sem["va"], 1)
-        for c0 in done:
-            if lo <= c0 < hi:
-                done[c0] = k
-    for c0, q, sem in ((0, g.sync, "sta"), (H, g.scalar, "stb")):
+        done[lo] = k
+    for c0, q, sem in ((H, g.sync, "stb"), (0, g.scalar, "sta")):
         q.wait_ge(T.sem["va"], done[c0])
         q.dma_start(T.y[:, c0:c0 + H], T.acc[:, c0:c0 + H]).then_inc(T.sem[sem], 16)
         q.wait_ge(T.sem[sem], 16)
     v.wait_ge(T.sem["va"], len(pieces) - 1)
 
 
-def helper(g, core, T, topo, e, ncopies, send):
-    half, dests = send
-    n = count(topo.mask(T.cores[e], core)) // ncopies
+def helper(g, core, T, topo, e, calls):
+    got = landing(calls, e, core)
     total = 0
-    for which, sem in ((0, "hc"), (1, "hs")):
-        g.wait_ge(T.sem[sem], n)
-        total += emit_send(g, T, topo, core, e, half, dests, which, T.sem[half + str(e)])
+    for call in calls[core]:
+        sem = semaphore(e, call[0][0])
+        g.wait_ge(T.sem[sem], got[sem])
+        total += issue(g, T, topo, e, call)
     g.wait_ge(T.sem["sent"], total)

from concourse.bass import DstId, RemoteDMATransfer
from concourse.mybir import dt, AluOpType, AxisListType, ActivationFunctionType

N = 6
NC = 512
H = NC // 2
Q = NC // 4
NCORES = 112
BIG = 1.0e29

SCRATCH = {
    "wb": ("sbuf", [128, 4 * NC], "bfloat16"),
    "xb": ("sbuf", [128, 512], "bfloat16"),
    "rb": ("sbuf", [128, 512], "bfloat16"),
    "wq": ("sbuf", [128, N * NC], "float8_e4m3fn_x4"),
    "ws": ("sbuf", [128, N * NC], "uint8"),
    "xq": ("sbuf", [128, 128], "float8_e4m3fn_x4"),
    "xs": ("sbuf", [128, 128], "uint8"),
    "rq": ("sbuf", [128, 128], "float8_e4m3fn_x4"),
    "rs": ("sbuf", [128, 128], "uint8"),
    "m1": ("sbuf", [128, 4], "float32"),
    "m2": ("sbuf", [128, 4], "float32"),
    "pen": ("sbuf", [128, 8], "float32"),
    "msk": ("sbuf", [128, 8], "float32"),
    "sel": ("sbuf", [128, 8], "float32"),
    "gate": ("sbuf", [128, 8], "float32"),
    "p": ("sbuf", [128, N * NC], "float32"),
    "acc": ("sbuf", [128, NC], "float32"),
    "lg": ("psum", [128, 512], "float32"),
    "ps": ("psum", [128, 512 * 7], "float32"),
}
PIECES = 2 * N
SEMAPHORES = (["lwa", "lwb", "lx", "lr", "qa", "qb", "qx", "tl", "vg", "gt", "va", "sent", "sta", "stb"]
              + ["%s%d" % (u, e) for u in "abs" for e in range(N)]
              + ["mm%d" % k for k in range(PIECES)] + ["pr%d" % k for k in range(PIECES)])
LANDS = {"c0": "a", "c1": "a", "c2": "b", "c3": "b", "s": "s"}


def groups(mask, parts):
    bits = [i for i in range(16) if mask >> i & 1]
    return [sum(1 << i for i in bits[k::parts]) for k in range(parts)]


def count(mask):
    return bin(mask).count("1")


def make_plan(T, topo):
    rank_chips = [topo.chip(c) for c in T.cores]
    taken, used = set(T.cores), set()
    plan = []

    def pick(cand):
        h = [h for h in cand if h not in taken][-1]
        taken.add(h)
        return h

    for e in range(N):
        c = T.cores[e]
        chip = topo.chip(c)
        others = [T.cores[(e + k) % N] for k in range(1, N)]
        near = [d for d in others if topo.same_plane(chip, topo.chip(d))]
        far = [d for d in others if d not in near]
        local = [h for h in range(NCORES) if topo.chip(h) == chip and h != c]
        ports = [h for h in local if all(topo.may_write(h, d) for d in far)]
        pa = [h for h in ports if topo.die(h) == topo.die(c)]
        pb = [h for h in ports if topo.die(h) != topo.die(c)]
        nb = [h for h in local if h not in ports and topo.die(h) != topo.die(c)]
        relay = {}
        for d in far:
            if not any(topo.mates(topo.chip(d), r) for r in rank_chips):
                relay[d] = pick([h for h in range(NCORES) if topo.mates(topo.chip(h), topo.chip(d))
                                 and topo.may_write(h, d) and topo.may_write(c, h)])
        rest = [d for d in far if d not in relay]
        on, out = topo.mask(c, pa[0]), topo.mask(c, near[0])
        if len(near) == 1:
            idle = [h for h in range(NCORES) if topo.same_plane(topo.chip(h), chip) and topo.chip(h) not in used
                    and not any(r == topo.chip(h) or topo.mates(r, topo.chip(h)) for r in rank_chips)
                    and all(topo.may_write(h, d) for d in far)]
            h0 = pick([h for h in idle if topo.die(h) != topo.die(c)])
            h2 = pick([h for h in idle if topo.chip(h) == topo.chip(h0) and topo.die(h) == topo.die(c)])
            used.add(topo.chip(h0))
            keeper, to0 = pa[0], far
            m0, m1 = groups(out, 2)
            m2, m3 = groups(on & ~out, 2)
            first = [("c0", m0, [h0]), ("c1", m1 | m2, [pb[0]])]
            second = [("c2", m0, [h2]), ("c3", m1, [pb[1]]), ("s", m2, [keeper]), ("c3", m3, [nb[0]])]
            last = [("c2", m0, near), ("c0", m1, near)]
        else:
            h0, h2, keeper, to0 = pa[0], pa[1], pb[1], others
            g2, g4 = groups(on, 2), groups(on, 4)
            first = [("c0", g2[0], [h0]), ("c1", g2[1], [pb[0]])]
            second = [("c2", g4[0], [h2]), ("c3", g4[1], [pb[1]]), ("s", g4[2], [keeper]), ("c3", g4[3], [nb[0]])]
            last = [("c2", out, near)]
        calls = {c: [first, second, [("s", out, list(relay.values()) + near)], last]}
        calls[h0] = [[("c0", out, to0)]]
        calls[pb[0]] = [[("c1", out, others)]]
        calls[h2] = [[("c2", out, far)]]
        calls[pb[1]] = [[("c3", out, far)]]
        calls[nb[0]] = [[("c3", out, near)]]
        calls.setdefault(keeper, []).append([("s", out, rest)])
        for d, h in relay.items():
            calls[h] = [[("s", topo.mask(h, d), [d])]]
        plan.append(calls)
    return plan


def view(T, e, unit):
    if unit == "s":
        return T.ws[:, e * NC:(e + 1) * NC]
    lo = e * NC + Q * int(unit[1])
    return T.wq[:, lo:lo + Q].bitcast(dt.uint8)


def dst_id(topo, d):
    rid, pid, _ = topo.addr(d)
    return DstId(rid=rid, pnc=pid)


def semaphore(e, unit):
    return LANDS[unit] + str(e)


def issue(g, T, topo, e, call):
    tr = []
    for unit, mask, dests in call:
        v = view(T, e, unit)
        tr.append(RemoteDMATransfer(dst_ids=[dst_id(topo, d) for d in dests], dma_engine_mask=mask,
                                    remote_sem=T.sem[semaphore(e, unit)], srcs=[v], dsts=[v for _ in dests]))
    g.remote_dma_fused(tr, local_sem=T.sem["sent"])
    return sum(count(m) for _, m, _ in call)


def landing(calls, e, core):
    got = {}
    for cs in calls.values():
        for call in cs:
            for unit, mask, dests in call:
                if core in dests:
                    s = semaphore(e, unit)
                    got[s] = got.get(s, 0) + count(mask)
    return got


def rank_program(g, core, T, topo):
    plan = make_plan(T, topo)
    rank = T.rank_of(core)
    if rank is None:
        for e in range(N):
            if core in plan[e]:
                helper(g, core, T, topo, e, plan[e])
        return
    e = rank

    for lo, hi, sem in ((0, 4 * H, "lwa"), (4 * H, 4 * NC, "lwb")):
        g.sync.dma_start(T.wb[0:64, lo:hi], T.w[0:64, lo:hi]).then_inc(T.sem[sem], 16)
        g.scalar.dma_start(T.wb[64:128, lo:hi], T.w[64:128, lo:hi]).then_inc(T.sem[sem], 16)
    g.sync.dma_start(T.xb[:], T.x[:]).then_inc(T.sem["lx"], 16)
    g.scalar.dma_start(T.rb[:], T.rt[:]).then_inc(T.sem["lr"], 16)

    v = g.vector
    for lo, sem, done in ((0, "lwa", "qa"), (H, "lwb", "qb")):
        v.wait_ge(T.sem[sem], 32)
        v.quantize_mx(T.wq[:, e * NC + lo:e * NC + lo + H], T.ws[:, e * NC + lo:e * NC + lo + H],
                      T.wb[:, 4 * lo:4 * (lo + H)]).then_inc(T.sem[done], 1)
    v.wait_ge(T.sem["lx"], 16)
    v.quantize_mx(T.xq[:], T.xs[:], T.xb[:]).then_inc(T.sem["qx"], 1)
    v.wait_ge(T.sem["lr"], 16)
    v.quantize_mx(T.rq[:], T.rs[:], T.rb[:]).then_inc(T.sem["qx"], 1)

    total = 0
    g.wait_ge(T.sem["qa"], 1)
    for k, call in enumerate(plan[e][core]):
        if k == 1:
            g.wait_ge(T.sem["qb"], 1)
        total += issue(g, T, topo, e, call)
    g.wait_ge(T.sem["sent"], total)

    pieces = [(e, 0, NC, [("qa", 1), ("qb", 1)])]
    for k in range(1, N):
        s = (e - k) % N
        got = landing(plan[s], s, core)
        ab = [(s, lo, lo + H, [("s%d" % s, got["s%d" % s]), (n, got[n])]) for lo, n in ((0, "a%d" % s), (H, "b%d" % s))]
        pieces += ab if k < 3 else ab[::-1]

    t = g.tensor
    t.wait_ge(T.sem["qx"], 2)
    t.matmul_mx(T.lg[:, 0:128], T.xq[:], T.xs[:], T.rq[:], T.rs[:], True, True).then_inc(T.sem["tl"], 1)
    waited = set()
    for k, (s, lo, hi, sems) in enumerate(pieces):
        for name, n in sems:
            if name not in waited:
                t.wait_ge(T.sem[name], n)
                waited.add(name)
        if k >= 7:
            t.wait_ge(T.sem["pr%d" % (k - 7)], 1)
        b = 512 * (k % 7)
        t.matmul_mx(T.ps[:, b:b + hi - lo], T.xq[:], T.xs[:], T.wq[:, s * NC + lo:s * NC + hi],
                    T.ws[:, s * NC + lo:s * NC + hi], True, True).then_inc(T.sem["mm%d" % k], 1)

    lg = T.lg[:, 0:N]
    v.wait_ge(T.sem["tl"], 1)
    v.tensor_reduce(T.m1[:, 0:1], lg, AxisListType.X, AluOpType.max).then_inc(T.sem["vg"], 1)
    v.wait_ge(T.sem["vg"], 1)
    v.tensor_scalar(T.pen[:, 0:N], lg, T.m1[:, 0:1], BIG, AluOpType.is_equal, AluOpType.mult).then_inc(T.sem["vg"], 1)
    v.wait_ge(T.sem["vg"], 2)
    v.tensor_tensor(T.msk[:, 0:N], lg, T.pen[:, 0:N], AluOpType.subtract).then_inc(T.sem["vg"], 1)
    v.wait_ge(T.sem["vg"], 3)
    v.tensor_reduce(T.m2[:, 0:1], T.msk[:, 0:N], AxisListType.X, AluOpType.max).then_inc(T.sem["vg"], 1)
    v.wait_ge(T.sem["vg"], 4)
    v.tensor_scalar(T.sel[:, 0:N], lg, T.m2[:, 0:1], None, AluOpType.is_ge).then_inc(T.sem["vg"], 1)
    v.wait_ge(T.sem["vg"], 5)
    v.tensor_tensor(T.gate[:, 0:N], lg, T.sel[:, 0:N], AluOpType.mult).then_inc(T.sem["gt"], 1)

    g.scalar.wait_ge(T.sem["gt"], 1)
    for k, (s, lo, hi, sems) in enumerate(pieces):
        g.scalar.wait_ge(T.sem["mm%d" % k], 1)
        b = 512 * (k % 7)
        out = T.acc[:, lo:hi] if k == 0 else T.p[:, s * NC + lo:s * NC + hi]
        g.scalar.activation(out, T.ps[:, b:b + hi - lo], ActivationFunctionType.Copy,
                            scale=T.gate[:, s:s + 1]).then_inc(T.sem["pr%d" % k], 1)
    done = {0: 0, H: 0}
    v.wait_ge(T.sem["pr0"], 1)
    for k, (s, lo, hi, sems) in enumerate(pieces[1:], 1):
        v.wait_ge(T.sem["pr%d" % k], 1)
        if done[lo]:
            v.wait_ge(T.sem["va"], done[lo])
        v.tensor_tensor(T.acc[:, lo:hi], T.acc[:, lo:hi], T.p[:, s * NC + lo:s * NC + hi],
                        AluOpType.add).then_inc(T.sem["va"], 1)
        done[lo] = k
    for c0, q, sem in ((H, g.sync, "stb"), (0, g.scalar, "sta")):
        q.wait_ge(T.sem["va"], done[c0])
        q.dma_start(T.y[:, c0:c0 + H], T.acc[:, c0:c0 + H]).then_inc(T.sem[sem], 16)
        q.wait_ge(T.sem[sem], 16)
    v.wait_ge(T.sem["va"], len(pieces) - 1)


def helper(g, core, T, topo, e, calls):
    got = landing(calls, e, core)
    total = 0
    for call in calls[core]:
        sem = semaphore(e, call[0][0])
        g.wait_ge(T.sem[sem], got[sem])
        total += issue(g, T, topo, e, call)
    g.wait_ge(T.sem["sent"], total)
